import numpy as np
import ml_dtypes


def mxq(x, axis, fmt="e4m3"):
    dtype, down = {"e4m3": (ml_dtypes.float8_e4m3fn, 7), "e5m2": (ml_dtypes.float8_e5m2, 14)}[fmt]
    v = np.moveaxis(np.asarray(x, np.float32).astype(ml_dtypes.bfloat16).astype(np.float64), axis, -1)
    blocks = v.reshape(v.shape[:-1] + (-1, 32))
    amax = np.abs(blocks).max(-1, keepdims=True)
    byte = np.maximum(np.where(amax > 0, np.frexp(amax)[1] - 1 + 127, 0) - down, 1)
    scale = np.exp2(byte - 127.0)
    codes = (blocks / scale).astype(np.float32).astype(dtype).astype(np.float64)
    return np.moveaxis((codes * scale).reshape(v.shape), -1, axis)


WIDE = False


def mx_kscale(k):
    if not WIDE:
        return np.ones(k)
    levels = np.array([10, -10, 5, -5, 0])
    if k % 512:
        return np.exp2(np.random.permutation(np.resize(levels, k // 32))).repeat(32)
    a = np.empty((k // 512, 16))
    for p in range(k // 512):
        a[p, :8] = np.random.permutation(np.resize(levels, 8))
        for g in range(8):
            far = levels[np.abs(levels - a[p, g]) >= 10]
            a[p, g + 8] = far[np.random.randint(len(far))]
    return np.exp2(a.ravel()).repeat(32)


def f64(x):
    return np.asarray(x).astype(np.float64)


def striped(idx):
    return np.tile(idx.reshape(-1, 16).T, (8, 1)).astype(np.uint16)


def unstriped(offs):
    return offs[:16].T.reshape(-1).astype(np.int64)


def pack_weight(w):
    k, n = w.shape
    w = f64(np.asarray(w, np.float32).astype(ml_dtypes.bfloat16)).reshape(k // 32, 32, n)
    amax = np.abs(w).max(1)
    byte = np.clip(np.where(amax > 0, np.frexp(amax)[1] - 1 + 127 - 7, 1), 1, 254)
    scaled = (w * np.exp2(127.0 - byte)[:, None, :]).reshape(k, n).astype(np.float32)
    words = np.ascontiguousarray(scaled.reshape(k // 512, 128, 4, n).transpose(0, 1, 3, 2)).astype(ml_dtypes.float8_e4m3fn).view(np.uint8)
    return words, np.ascontiguousarray(byte.astype(np.uint8).reshape(k // 512, 16, n))


def unpack_weight(words, scales):
    g, p, n, _ = words.shape
    vals = np.ascontiguousarray(words).view(ml_dtypes.float8_e4m3fn).astype(np.float64) * np.repeat(np.exp2(scales.astype(np.float64) - 127.0), 8, axis=1)[..., None]
    return vals.transpose(0, 1, 3, 2).reshape(g * 512, n)


def sigmoid(v):
    return 1.0 / (1.0 + np.exp(-np.maximum(v, -700.0)))


K, T, S, N, H, W = 512, 2048, 512, 128, 512, 2048


def setup_inputs():
    n = np.random.standard_normal
    s = mx_kscale(K)[:, None]
    u = mx_kscale(H)
    packed_xT = pack_weight(n((K, T)) * s)
    packed_eT = pack_weight(n((K, W)) * s)
    return {
        "x_words": packed_xT[0],
        "x_scales": packed_xT[1],
        "w1": (n((K, H)) / np.sqrt(K) / s).astype(np.float32),
        "e_words": packed_eT[0],
        "e_scales": packed_eT[1],
        "w2": (n((K, H)) / np.sqrt(K) / s).astype(np.float32),
        "unit": (np.random.uniform(0.6, 1.4, (H, 1)) * u[:, None]).astype(np.float32),
        "w3": (n((H, N)) / np.sqrt(H) / u[:, None]).astype(np.float32),
        "offs": striped(np.random.permutation(T)[:S]),
        "fresh": striped(np.random.permutation(W)[:S]),
    }


def reference(x_words, x_scales, w1, e_words, e_scales, w2, unit, w3, offs, fresh):
    xq = unpack_weight(x_words, x_scales)[:, unstriped(offs)]
    y = mxq(f64(w1), 0, "e4m3").T @ xq
    e_fresh = unpack_weight(e_words, e_scales)[:, unstriped(fresh)]
    ye = mxq(f64(w2), 0, "e4m3").T @ e_fresh
    dev = np.abs(ye - y)
    avg = dev.mean(axis=1, keepdims=True)
    rel = dev / (avg + 0.2)
    alp = sigmoid(3.0 * rel - 3.0)
    bld = y + alp * (ye - y)
    hid = f64(unit) * bld
    return mxq(f64(w3), 0, "e4m3").T @ mxq(hid, 0, "e4m3")

@@ -1,0 +1,227 @@
+from contextlib import ExitStack
+
+import concourse.mybir as mybir
+
+K, T, S, N, H = 512, 2048, 512, 128, 512
+FLOPS = 2 * K * H * S * 2 + 2 * H * N * S
+
+F32 = mybir.dt.float32
+BF16 = mybir.dt.bfloat16
+I32 = mybir.dt.int32
+U32 = mybir.dt.uint32
+U16 = mybir.dt.uint16
+U8 = mybir.dt.uint8
+FP8X4 = mybir.dt.float8_e4m3fn_x4
+ALU = mybir.AluOpType
+ACT = mybir.ActivationFunctionType
+
+P = 128
+PACK = 4
+IN_PSUM = (0, 1)
+IN_SBUF = (2, 3)
+CHUNKS = ((0, 256), (256, 384), (384, 512))
+
+
+def tile_picked_ycblnd_blend_p_kernel(tc, x_words, x_scales, w1, e_words, e_scales, w2, unit, w3, offs, fresh, out):
+    nc = tc.nc
+    with ExitStack() as ctx:
+        sb = ctx.enter_context(tc.tile_pool(name="sb", bufs=1))
+        ps = ctx.enter_context(tc.psum_pool(name="ps", bufs=1))
+
+        def scale_table(name):
+            tile = sb.tile([P, T], U8, name=name, align_bytes=64)
+            nc.vector.memset(tile[:].bitcast(I32), 0)
+            return tile
+
+        def load_scales(tile, scales):
+            for q in range(4):
+                nc.sync.dma_start(out=tile[32 * q : 32 * q + 4, :].bitcast(I32), in_=scales[0, 4 * q : 4 * q + 4, :].bitcast(I32))
+
+        def load_words(name, words):
+            tile = sb.tile([P, T], I32, name=name, align_bytes=64)
+            nc.sync.dma_start(out=tile[:], in_=words[0].rearrange("p n r -> p (n r)").bitcast(I32))
+            return tile
+
+        def load_list(name, src):
+            tile = sb.tile([P, S // 16], U16, name=name)
+            nc.sync.dma_start(tile[:], src)
+            return tile
+
+        def load_weight(name, w):
+            tile = sb.tile([P, PACK, H], F32, name=name, align_bytes=64)
+            nc.sync.dma_start(out=tile[:], in_=w.rearrange("(p j) c -> p j c", j=PACK))
+            return tile
+
+        xs_tab = scale_table("xs_tab")
+        es_tab = scale_table("es_tab")
+        minus3 = sb.tile([P, 1], F32, name="minus3")
+        nc.vector.memset(minus3[:], -3.0)
+
+        offs_t = load_list("offs_t", offs)
+        xw_tab = load_words("xw_tab", x_words)
+        load_scales(xs_tab, x_scales)
+        fresh_t = load_list("fresh_t", fresh)
+        w1_raw = load_weight("w1_raw", w1)
+        w2_raw = load_weight("w2_raw", w2)
+        load_scales(es_tab, e_scales)
+        unit_t = sb.tile([P, 2 * PACK], F32, name="unit_t")
+        unit_rows = unit.rearrange("(mm e) o -> mm (e o)", e=2 * PACK)
+        for u in range(2):
+            nc.sync.dma_start(out=unit_t[u:P:2, 0:7], in_=unit_rows[:, u : u + 7])
+        ew_tab = load_words("ew_tab", e_words)
+        w3_raw = sb.tile([P, PACK, N], F32, name="w3_raw", align_bytes=64)
+        w3_rows = w3.rearrange("(mm t u) n -> u mm t n", t=PACK, u=2)
+        for u in range(2):
+            nc.sync.dma_start(out=w3_raw[u:P:2, :, :], in_=w3_rows[u])
+
+        xs = sb.tile([P, S], U8, name="xs", align_bytes=64)
+        xw = sb.tile([P, S], U32, name="xw", align_bytes=64)
+        es = sb.tile([P, S], U8, name="es", align_bytes=64)
+        nc.vector.tensor_copy(out=xs[:], in_=xs_tab[:].indirect(offs_t[:]))
+        nc.vector.tensor_copy(out=xw[:], in_=xw_tab[:].bitcast(U32).indirect(offs_t[:]))
+
+        def deal(raw, t, name):
+            grouped = sb.tile([P, P, PACK], BF16, name=name, align_bytes=64)
+            src = raw[:].rearrange("p j (mm t u) -> p j mm t u", t=PACK, u=2)[:, :, :, t, :].rearrange("p j mm u -> p mm j u")
+            dst = grouped[:].rearrange("p (mm u) j -> p mm j u", u=2)
+            return grouped, src, dst
+
+        def quantize(grouped, cols, name):
+            codes = sb.tile([P, cols], U32, name=name + "_codes", align_bytes=64)
+            plane = sb.tile([P, cols], U8, name=name + "_plane", align_bytes=64)
+            nc.vector.quantize_mx(out=codes[:].bitcast(FP8X4), scales=plane[:], in_=grouped)
+            return codes, plane
+
+        w1_grouped = {}
+        for t in IN_SBUF + IN_PSUM:
+            grouped, src, dst = deal(w1_raw, t, "w1_grouped%d" % t)
+            if t in IN_SBUF:
+                nc.vector.tensor_scalar(out=dst, in0=src, scalar1=-1.0, scalar2=None, op0=ALU.mult)
+            else:
+                nc.scalar.activation(out=dst, in_=src, func=ACT.Copy, scale=-1.0)
+            w1_grouped[t] = grouped
+        w1_q = {}
+        for t in IN_SBUF + IN_PSUM:
+            w1_q[t] = quantize(w1_grouped[t][:].rearrange("p m j -> p (m j)"), P, "w1q%d" % t)
+
+        def product(bank, wq, words, plane, start, stop):
+            nc.tensor.matmul_mx(out=bank, lhsT=wq[0][:].bitcast(FP8X4), lhsT_scale=wq[1][:], rhs=words.bitcast(FP8X4), rhs_scale=plane, start=start, stop=stop)
+
+        neg_y_bank = {}
+        for t in IN_SBUF + IN_PSUM:
+            neg_y_bank[t] = ps.tile([P, S], F32, name="neg_y_bank%d" % t, tag="first%d" % t)
+            product(neg_y_bank[t][:], w1_q[t], xw[:], xs[:], True, True)
+        second = {}
+        for t in range(PACK):
+            second[t] = ps.tile([P, S], F32, name="second%d" % t)
+        for t in IN_PSUM:
+            product(second[t][:], w1_q[t], xw[:], xs[:], True, False)
+
+        neg_y = {}
+        for t in IN_SBUF:
+            neg_y[t] = sb.tile([P, S], F32, name="neg_y%d" % t)
+            nc.scalar.copy(out=neg_y[t][:], in_=neg_y_bank[t][:])
+        neg_uy = sb.tile([P, PACK, S], F32, name="neg_uy")
+        for t in IN_SBUF + IN_PSUM:
+            nc.scalar.activation(out=neg_uy[:, t, :], in_=neg_y_bank[t][:], func=ACT.Copy, scale=unit_t[:, 2 * t : 2 * t + 1])
+
+        nc.vector.tensor_copy(out=es[:], in_=es_tab[:].indirect(fresh_t[:]))
+        w2_grouped = {}
+        for t in range(PACK):
+            grouped, src, dst = deal(w2_raw, t, "w2_grouped%d" % t)
+            nc.vector.tensor_copy(out=dst, in_=src)
+            w2_grouped[t] = grouped
+        w2_q = {}
+        for t in range(PACK):
+            w2_q[t] = quantize(w2_grouped[t][:].rearrange("p m j -> p (m j)"), P, "w2q%d" % t)
+
+        half = S // 2
+        for h in range(2):
+            ew = sb.tile([P, half], U32, name="ew%d" % h, align_bytes=64)
+            nc.vector.tensor_copy(out=ew[:], in_=ew_tab[:].bitcast(U32).indirect(fresh_t[:, h * half // 16 : (h + 1) * half // 16]))
+            cols = slice(h * half, (h + 1) * half)
+            for t in (0, 2, 1, 3):
+                in_psum = t in IN_PSUM
+                product(second[t][:, cols], w2_q[t], ew[:], es[:, cols], not in_psum, (not in_psum) or h == 1)
+
+        diff = {}
+        dev = {}
+        alp = {}
+        dev_sum = sb.tile([P, PACK], F32, name="dev_sum")
+        denom = sb.tile([P, PACK], F32, name="denom")
+        slope = sb.tile([P, PACK], F32, name="slope")
+        moved = sb.tile([P, PACK, S], F32, name="moved")
+        for t in range(PACK):
+            dev[t] = sb.tile([P, S], F32, name="dev%d" % t)
+            alp[t] = sb.tile([P, S], F32, name="alp%d" % t)
+        for t in IN_PSUM:
+            diff[t] = second[t]
+
+        def subtract(t):
+            diff[t] = sb.tile([P, S], F32, name="diff%d" % t)
+            nc.vector.tensor_tensor(out=diff[t][:], in0=second[t][:], in1=neg_y[t][:], op=ALU.add)
+
+        def abs_scalar(t):
+            nc.scalar.activation(out=dev[t][:], in_=diff[t][:], func=ACT.Abs, accum_out=dev_sum[:, t : t + 1])
+
+        def abs_vector(t):
+            nc.vector.scalar_tensor_tensor(out=dev[t][:], in0=diff[t][:], scalar=-1.0, in1=diff[t][:], op0=ALU.mult, op1=ALU.max, accum_out=dev_sum[:, t : t + 1])
+
+        def row_slope(lo, hi):
+            nc.vector.tensor_scalar(out=denom[:, lo:hi], in0=dev_sum[:, lo:hi], scalar1=1.0 / (3.0 * S), scalar2=0.2 / 3.0, op0=ALU.mult, op1=ALU.add)
+            nc.vector.reciprocal(out=slope[:, lo:hi], in_=denom[:, lo:hi])
+
+        def gate(t):
+            nc.scalar.activation(out=alp[t][:], in_=dev[t][:], func=ACT.Sigmoid, bias=minus3[:], scale=slope[:, t : t + 1])
+
+        def move(t):
+            nc.vector.scalar_tensor_tensor(out=moved[:, t, :], in0=diff[t][:], scalar=unit_t[:, 2 * t : 2 * t + 1], in1=alp[t][:], op0=ALU.mult, op1=ALU.mult)
+
+        abs_scalar(0)
+        subtract(2)
+        row_slope(0, 1)
+        abs_scalar(1)
+        subtract(3)
+        row_slope(1, 2)
+        gate(0)
+        abs_vector(3)
+        abs_scalar(2)
+        gate(1)
+        move(0)
+        row_slope(2, 4)
+        gate(2)
+        gate(3)
+        move(1)
+
+        w3_grouped = sb.tile([P, N, PACK], BF16, name="w3_grouped", align_bytes=64)
+        nc.vector.tensor_copy(
+            out=w3_grouped[:].rearrange("p (c i) t -> p c t i", i=2),
+            in_=w3_raw[:].rearrange("p t (c i) -> p c t i", i=2),
+        )
+        move(2)
+        w3_q = quantize(w3_grouped[:].rearrange("p n t -> p (n t)"), N, "w3q")
+        move(3)
+
+        hid = []
+        for c, (lo, hi) in enumerate(CHUNKS):
+            tile = sb.tile([P, hi - lo, PACK], BF16, name="hid%d" % c, align_bytes=64)
+            nc.vector.tensor_tensor(
+                out=tile[:].rearrange("p (c i) t -> p c t i", i=2),
+                in0=moved[:, :, lo:hi].rearrange("p t (c i) -> p c t i", i=2),
+                in1=neg_uy[:, :, lo:hi].rearrange("p t (c i) -> p c t i", i=2),
+                op=ALU.subtract,
+            )
+            hid.append(tile)
+            if c > 0:
+                finish(nc, sb, ps, c - 1, hid, w3_q, quantize, product, out)
+        finish(nc, sb, ps, len(CHUNKS) - 1, hid, w3_q, quantize, product, out)
+
+
+def finish(nc, sb, ps, c, hid, w3_q, quantize, product, out):
+    lo, hi = CHUNKS[c]
+    codes, plane = quantize(hid[c][:].rearrange("p n t -> p (n t)"), hi - lo, "hidq%d" % c)
+    bank = ps.tile([P, S], F32, name="out_bank%d" % c, tag="first%d" % c)
+    product(bank[:, 0 : hi - lo], w3_q, codes[:], plane[:], True, True)
+    result = sb.tile([P, hi - lo], F32, name="result%d" % c)
+    nc.scalar.copy(out=result[:], in_=bank[:, 0 : hi - lo])
+    nc.sync.dma_start(out=out[:, lo:hi], in_=result[:])

@@ -29,13 +29,13 @@ def tile_picked_ycblnd_blend_p_kernel(tc, x_words, x_scales, w1, e_words, e_scal
         ps = ctx.enter_context(tc.psum_pool(name="ps", bufs=1))
 
         def scale_table(name):
-            tile = sb.tile([P, T], U8, name=name, align_bytes=64)
+            tile = sb.tile([P, T], U8, name=name, tag=name, align_bytes=64)
             nc.vector.memset(tile[:].bitcast(I32), 0)
             return tile
 
-        def load_scales(tile, scales):
+        def load_scales(queue, tile, scales, first):
             for q in range(4):
-                nc.sync.dma_start(out=tile[32 * q : 32 * q + 4, :].bitcast(I32), in_=scales[0, 4 * q : 4 * q + 4, :].bitcast(I32))
+                queue.dma_start(out=tile[32 * q + first : 32 * q + first + 4, :].bitcast(I32), in_=scales[0, 4 * q : 4 * q + 4, :].bitcast(I32))
 
         def load_words(name, words):
             tile = sb.tile([P, T], I32, name=name, align_bytes=64)
@@ -48,7 +48,7 @@ def tile_picked_ycblnd_blend_p_kernel(tc, x_words, x_scales, w1, e_words, e_scal
             return tile
 
         def load_weight(name, w):
-            tile = sb.tile([P, PACK, H], F32, name=name, align_bytes=64)
+            tile = sb.tile([P, PACK, H], F32, name=name, tag=name, align_bytes=64)
             nc.sync.dma_start(out=tile[:], in_=w.rearrange("(p j) c -> p j c", j=PACK))
             return tile
 
@@ -57,28 +57,29 @@ def tile_picked_ycblnd_blend_p_kernel(tc, x_words, x_scales, w1, e_words, e_scal
         minus3 = sb.tile([P, 1], F32, name="minus3")
         nc.vector.memset(minus3[:], -3.0)
 
+        warm = sb.tile([P, 1], F32, name="warm")
+        nc.scalar.activation(out=warm[:], in_=minus3[:], func=ACT.Sigmoid, bias=minus3[:], scale=1.0)
         offs_t = load_list("offs_t", offs)
-        xw_tab = load_words("xw_tab", x_words)
-        load_scales(xs_tab, x_scales)
-        fresh_t = load_list("fresh_t", fresh)
         w1_raw = load_weight("w1_raw", w1)
-        w2_raw = load_weight("w2_raw", w2)
-        load_scales(es_tab, e_scales)
+        fresh_t = load_list("fresh_t", fresh)
         unit_t = sb.tile([P, 2 * PACK], F32, name="unit_t")
         unit_rows = unit.rearrange("(mm e) o -> mm (e o)", e=2 * PACK)
-        for u in range(2):
+
+        def load_unit(u):
             nc.sync.dma_start(out=unit_t[u:P:2, 0:7], in_=unit_rows[:, u : u + 7])
+
+        load_unit(0)
+        load_scales(nc.sync, xs_tab, x_scales, 0)
+        xw_tab = load_words("xw_tab", x_words)
+        load_scales(nc.sync, es_tab, e_scales, 8)
+        w2_raw = load_weight("w2_raw", w2)
+        load_unit(1)
         ew_tab = load_words("ew_tab", e_words)
-        w3_raw = sb.tile([P, PACK, N], F32, name="w3_raw", align_bytes=64)
-        w3_rows = w3.rearrange("(mm t u) n -> u mm t n", t=PACK, u=2)
-        for u in range(2):
-            nc.sync.dma_start(out=w3_raw[u:P:2, :, :], in_=w3_rows[u])
 
         xs = sb.tile([P, S], U8, name="xs", align_bytes=64)
         xw = sb.tile([P, S], U32, name="xw", align_bytes=64)
         es = sb.tile([P, S], U8, name="es", align_bytes=64)
         nc.vector.tensor_copy(out=xs[:], in_=xs_tab[:].indirect(offs_t[:]))
-        nc.vector.tensor_copy(out=xw[:], in_=xw_tab[:].bitcast(U32).indirect(offs_t[:]))
 
         def deal(raw, t, name):
             grouped = sb.tile([P, P, PACK], BF16, name=name, align_bytes=64)
@@ -90,22 +91,25 @@ def tile_picked_ycblnd_blend_p_kernel(tc, x_words, x_scales, w1, e_words, e_scal
             codes = sb.tile([P, cols], U32, name=name + "_codes", align_bytes=64)
             plane = sb.tile([P, cols], U8, name=name + "_plane", align_bytes=64)
             nc.vector.quantize_mx(out=codes[:].bitcast(FP8X4), scales=plane[:], in_=grouped)
-            return codes, plane
+            return codes[:], plane[:]
 
         w1_grouped = {}
         for t in IN_SBUF + IN_PSUM:
             grouped, src, dst = deal(w1_raw, t, "w1_grouped%d" % t)
-            if t in IN_SBUF:
-                nc.vector.tensor_scalar(out=dst, in0=src, scalar1=-1.0, scalar2=None, op0=ALU.mult)
-            else:
-                nc.scalar.activation(out=dst, in_=src, func=ACT.Copy, scale=-1.0)
+            nc.scalar.activation(out=dst, in_=src, func=ACT.Copy, scale=-1.0)
             w1_grouped[t] = grouped
         w1_q = {}
+        w1_codes = sb.tile([P, H], U32, name="w1_codes", tag="xs_tab", align_bytes=64)
+        w1_plane = sb.tile([P, H], U8, name="w1_plane", align_bytes=64)
         for t in IN_SBUF + IN_PSUM:
-            w1_q[t] = quantize(w1_grouped[t][:].rearrange("p m j -> p (m j)"), P, "w1q%d" % t)
+            cols = slice(t * P, (t + 1) * P)
+            nc.vector.quantize_mx(out=w1_codes[:, cols].bitcast(FP8X4), scales=w1_plane[:, cols], in_=w1_grouped[t][:].rearrange("p m j -> p (m j)"))
+            w1_q[t] = (w1_codes[:, cols], w1_plane[:, cols])
+
+        nc.vector.tensor_copy(out=xw[:], in_=xw_tab[:].bitcast(U32).indirect(offs_t[:]))
 
         def product(bank, wq, words, plane, start, stop):
-            nc.tensor.matmul_mx(out=bank, lhsT=wq[0][:].bitcast(FP8X4), lhsT_scale=wq[1][:], rhs=words.bitcast(FP8X4), rhs_scale=plane, start=start, stop=stop)
+            nc.tensor.matmul_mx(out=bank, lhsT=wq[0].bitcast(FP8X4), lhsT_scale=wq[1], rhs=words.bitcast(FP8X4), rhs_scale=plane, start=start, stop=stop)
 
         neg_y_bank = {}
         for t in IN_SBUF + IN_PSUM:
@@ -135,6 +139,11 @@ def tile_picked_ycblnd_blend_p_kernel(tc, x_words, x_scales, w1, e_words, e_scal
         for t in range(PACK):
             w2_q[t] = quantize(w2_grouped[t][:].rearrange("p m j -> p (m j)"), P, "w2q%d" % t)
 
+        w3_raw = sb.tile([P, PACK, N], F32, name="w3_raw", tag="w2_raw", align_bytes=64)
+        w3_rows = w3.rearrange("(mm t u) n -> u mm t n", t=PACK, u=2)
+        for u in range(2):
+            nc.sync.dma_start(out=w3_raw[u:P:2, :, :], in_=w3_rows[u])
+
         half = S // 2
         for h in range(2):
             ew = sb.tile([P, half], U32, name="ew%d" % h, align_bytes=64)
@@ -142,7 +151,7 @@ def tile_picked_ycblnd_blend_p_kernel(tc, x_words, x_scales, w1, e_words, e_scal
             cols = slice(h * half, (h + 1) * half)
             for t in (0, 2, 1, 3):
                 in_psum = t in IN_PSUM
-                product(second[t][:, cols], w2_q[t], ew[:], es[:, cols], not in_psum, (not in_psum) or h == 1)
+                product(second[t][:, cols], w2_q[t], ew[:], es[8:P, cols], not in_psum, (not in_psum) or h == 1)
 
         diff = {}
         dev = {}
@@ -189,26 +198,26 @@ def tile_picked_ycblnd_blend_p_kernel(tc, x_words, x_scales, w1, e_words, e_scal
         gate(1)
         move(0)
         row_slope(2, 4)
-        gate(2)
         gate(3)
+        gate(2)
         move(1)
 
         w3_grouped = sb.tile([P, N, PACK], BF16, name="w3_grouped", align_bytes=64)
-        nc.vector.tensor_copy(
-            out=w3_grouped[:].rearrange("p (c i) t -> p c t i", i=2),
-            in_=w3_raw[:].rearrange("p t (c i) -> p c t i", i=2),
+        nc.scalar.copy(
+            out=w3_grouped[:].rearrange("p (c i) t -> p c t i", i=4),
+            in_=w3_raw[:].rearrange("p t (c i) -> p c t i", i=4),
         )
+        move(3)
         move(2)
         w3_q = quantize(w3_grouped[:].rearrange("p n t -> p (n t)"), N, "w3q")
-        move(3)
 
         hid = []
         for c, (lo, hi) in enumerate(CHUNKS):
             tile = sb.tile([P, hi - lo, PACK], BF16, name="hid%d" % c, align_bytes=64)
             nc.vector.tensor_tensor(
-                out=tile[:].rearrange("p (c i) t -> p c t i", i=2),
-                in0=moved[:, :, lo:hi].rearrange("p t (c i) -> p c t i", i=2),
-                in1=neg_uy[:, :, lo:hi].rearrange("p t (c i) -> p c t i", i=2),
+                out=tile[:].rearrange("p (c i) t -> p c t i", i=4),
+                in0=moved[:, :, lo:hi].rearrange("p t (c i) -> p c t i", i=4),
+                in1=neg_uy[:, :, lo:hi].rearrange("p t (c i) -> p c t i", i=4),
                 op=ALU.subtract,
             )
             hid.append(tile)
@@ -221,7 +230,7 @@ def finish(nc, sb, ps, c, hid, w3_q, quantize, product, out):
     lo, hi = CHUNKS[c]
     codes, plane = quantize(hid[c][:].rearrange("p n t -> p (n t)"), hi - lo, "hidq%d" % c)
     bank = ps.tile([P, S], F32, name="out_bank%d" % c, tag="first%d" % c)
-    product(bank[:, 0 : hi - lo], w3_q, codes[:], plane[:], True, True)
+    product(bank[:, 0 : hi - lo], w3_q, codes, plane, True, True)
     result = sb.tile([P, hi - lo], F32, name="result%d" % c)
     nc.scalar.copy(out=result[:], in_=bank[:, 0 : hi - lo])
     nc.sync.dma_start(out=out[:, lo:hi], in_=result[:])

from contextlib import ExitStack

import concourse.mybir as mybir

K, T, S, N, H = 512, 2048, 512, 128, 512
FLOPS = 2 * K * H * S * 2 + 2 * H * N * S

F32 = mybir.dt.float32
BF16 = mybir.dt.bfloat16
I32 = mybir.dt.int32
U32 = mybir.dt.uint32
U16 = mybir.dt.uint16
U8 = mybir.dt.uint8
FP8X4 = mybir.dt.float8_e4m3fn_x4
ALU = mybir.AluOpType
ACT = mybir.ActivationFunctionType

P = 128
PACK = 4
IN_PSUM = (0, 1)
IN_SBUF = (2, 3)
CHUNKS = ((0, 256), (256, 384), (384, 512))


def tile_picked_ycblnd_blend_p_kernel(tc, x_words, x_scales, w1, e_words, e_scales, w2, unit, w3, offs, fresh, out):
    nc = tc.nc
    with ExitStack() as ctx:
        sb = ctx.enter_context(tc.tile_pool(name="sb", bufs=1))
        ps = ctx.enter_context(tc.psum_pool(name="ps", bufs=1))

        def scale_table(name):
            tile = sb.tile([P, T], U8, name=name, tag=name, align_bytes=64)
            nc.vector.memset(tile[:].bitcast(I32), 0)
            return tile

        def load_scales(queue, tile, scales, first):
            for q in range(4):
                queue.dma_start(out=tile[32 * q + first : 32 * q + first + 4, :].bitcast(I32), in_=scales[0, 4 * q : 4 * q + 4, :].bitcast(I32))

        def load_words(name, words):
            tile = sb.tile([P, T], I32, name=name, align_bytes=64)
            nc.sync.dma_start(out=tile[:], in_=words[0].rearrange("p n r -> p (n r)").bitcast(I32))
            return tile

        def load_list(name, src):
            tile = sb.tile([P, S // 16], U16, name=name)
            nc.sync.dma_start(tile[:], src)
            return tile

        def load_weight(name, w):
            tile = sb.tile([P, PACK, H], F32, name=name, tag=name, align_bytes=64)
            nc.sync.dma_start(out=tile[:], in_=w.rearrange("(p j) c -> p j c", j=PACK))
            return tile

        xs_tab = scale_table("xs_tab")
        es_tab = scale_table("es_tab")
        minus3 = sb.tile([P, 1], F32, name="minus3")
        nc.vector.memset(minus3[:], -3.0)

        warm = sb.tile([P, 1], F32, name="warm")
        nc.scalar.activation(out=warm[:], in_=minus3[:], func=ACT.Sigmoid, bias=minus3[:], scale=1.0)
        offs_t = load_list("offs_t", offs)
        w1_raw = load_weight("w1_raw", w1)
        fresh_t = load_list("fresh_t", fresh)
        unit_t = sb.tile([P, 2 * PACK], F32, name="unit_t")
        unit_rows = unit.rearrange("(mm e) o -> mm (e o)", e=2 * PACK)

        def load_unit(u):
            nc.sync.dma_start(out=unit_t[u:P:2, 0:7], in_=unit_rows[:, u : u + 7])

        load_unit(0)
        load_scales(nc.sync, xs_tab, x_scales, 0)
        xw_tab = load_words("xw_tab", x_words)
        load_scales(nc.sync, es_tab, e_scales, 8)
        w2_raw = load_weight("w2_raw", w2)
        load_unit(1)
        ew_tab = load_words("ew_tab", e_words)

        xs = sb.tile([P, S], U8, name="xs", align_bytes=64)
        xw = sb.tile([P, S], U32, name="xw", align_bytes=64)
        es = sb.tile([P, S], U8, name="es", align_bytes=64)
        nc.vector.tensor_copy(out=xs[:], in_=xs_tab[:].indirect(offs_t[:]))

        def deal(raw, t, name):
            grouped = sb.tile([P, P, PACK], BF16, name=name, align_bytes=64)
            src = raw[:].rearrange("p j (mm t u) -> p j mm t u", t=PACK, u=2)[:, :, :, t, :].rearrange("p j mm u -> p mm j u")
            dst = grouped[:].rearrange("p (mm u) j -> p mm j u", u=2)
            return grouped, src, dst

        def quantize(grouped, cols, name):
            codes = sb.tile([P, cols], U32, name=name + "_codes", align_bytes=64)
            plane = sb.tile([P, cols], U8, name=name + "_plane", align_bytes=64)
            nc.vector.quantize_mx(out=codes[:].bitcast(FP8X4), scales=plane[:], in_=grouped)
            return codes[:], plane[:]

        w1_grouped = {}
        for t in IN_SBUF + IN_PSUM:
            grouped, src, dst = deal(w1_raw, t, "w1_grouped%d" % t)
            nc.scalar.activation(out=dst, in_=src, func=ACT.Copy, scale=-1.0)
            w1_grouped[t] = grouped
        w1_q = {}
        w1_codes = sb.tile([P, H], U32, name="w1_codes", tag="xs_tab", align_bytes=64)
        w1_plane = sb.tile([P, H], U8, name="w1_plane", align_bytes=64)
        for t in IN_SBUF + IN_PSUM:
            cols = slice(t * P, (t + 1) * P)
            nc.vector.quantize_mx(out=w1_codes[:, cols].bitcast(FP8X4), scales=w1_plane[:, cols], in_=w1_grouped[t][:].rearrange("p m j -> p (m j)"))
            w1_q[t] = (w1_codes[:, cols], w1_plane[:, cols])

        nc.vector.tensor_copy(out=xw[:], in_=xw_tab[:].bitcast(U32).indirect(offs_t[:]))

        def product(bank, wq, words, plane, start, stop):
            nc.tensor.matmul_mx(out=bank, lhsT=wq[0].bitcast(FP8X4), lhsT_scale=wq[1], rhs=words.bitcast(FP8X4), rhs_scale=plane, start=start, stop=stop)

        neg_y_bank = {}
        for t in IN_SBUF + IN_PSUM:
            neg_y_bank[t] = ps.tile([P, S], F32, name="neg_y_bank%d" % t, tag="first%d" % t)
            product(neg_y_bank[t][:], w1_q[t], xw[:], xs[:], True, True)
        second = {}
        for t in range(PACK):
            second[t] = ps.tile([P, S], F32, name="second%d" % t)
        for t in IN_PSUM:
            product(second[t][:], w1_q[t], xw[:], xs[:], True, False)

        neg_y = {}
        for t in IN_SBUF:
            neg_y[t] = sb.tile([P, S], F32, name="neg_y%d" % t)
            nc.scalar.copy(out=neg_y[t][:], in_=neg_y_bank[t][:])
        neg_uy = sb.tile([P, PACK, S], F32, name="neg_uy")
        for t in IN_SBUF + IN_PSUM:
            nc.scalar.activation(out=neg_uy[:, t, :], in_=neg_y_bank[t][:], func=ACT.Copy, scale=unit_t[:, 2 * t : 2 * t + 1])

        nc.vector.tensor_copy(out=es[:], in_=es_tab[:].indirect(fresh_t[:]))
        w2_grouped = {}
        for t in range(PACK):
            grouped, src, dst = deal(w2_raw, t, "w2_grouped%d" % t)
            nc.vector.tensor_copy(out=dst, in_=src)
            w2_grouped[t] = grouped
        w2_q = {}
        for t in range(PACK):
            w2_q[t] = quantize(w2_grouped[t][:].rearrange("p m j -> p (m j)"), P, "w2q%d" % t)

        w3_raw = sb.tile([P, PACK, N], F32, name="w3_raw", tag="w2_raw", align_bytes=64)
        w3_rows = w3.rearrange("(mm t u) n -> u mm t n", t=PACK, u=2)
        for u in range(2):
            nc.sync.dma_start(out=w3_raw[u:P:2, :, :], in_=w3_rows[u])

        half = S // 2
        for h in range(2):
            ew = sb.tile([P, half], U32, name="ew%d" % h, align_bytes=64)
            nc.vector.tensor_copy(out=ew[:], in_=ew_tab[:].bitcast(U32).indirect(fresh_t[:, h * half // 16 : (h + 1) * half // 16]))
            cols = slice(h * half, (h + 1) * half)
            for t in (0, 2, 1, 3):
                in_psum = t in IN_PSUM
                product(second[t][:, cols], w2_q[t], ew[:], es[8:P, cols], not in_psum, (not in_psum) or h == 1)

        diff = {}
        dev = {}
        alp = {}
        dev_sum = sb.tile([P, PACK], F32, name="dev_sum")
        denom = sb.tile([P, PACK], F32, name="denom")
        slope = sb.tile([P, PACK], F32, name="slope")
        moved = sb.tile([P, PACK, S], F32, name="moved")
        for t in range(PACK):
            dev[t] = sb.tile([P, S], F32, name="dev%d" % t)
            alp[t] = sb.tile([P, S], F32, name="alp%d" % t)
        for t in IN_PSUM:
            diff[t] = second[t]

        def subtract(t):
            diff[t] = sb.tile([P, S], F32, name="diff%d" % t)
            nc.vector.tensor_tensor(out=diff[t][:], in0=second[t][:], in1=neg_y[t][:], op=ALU.add)

        def abs_scalar(t):
            nc.scalar.activation(out=dev[t][:], in_=diff[t][:], func=ACT.Abs, accum_out=dev_sum[:, t : t + 1])

        def abs_vector(t):
            nc.vector.scalar_tensor_tensor(out=dev[t][:], in0=diff[t][:], scalar=-1.0, in1=diff[t][:], op0=ALU.mult, op1=ALU.max, accum_out=dev_sum[:, t : t + 1])

        def row_slope(lo, hi):
            nc.vector.tensor_scalar(out=denom[:, lo:hi], in0=dev_sum[:, lo:hi], scalar1=1.0 / (3.0 * S), scalar2=0.2 / 3.0, op0=ALU.mult, op1=ALU.add)
            nc.vector.reciprocal(out=slope[:, lo:hi], in_=denom[:, lo:hi])

        def gate(t):
            nc.scalar.activation(out=alp[t][:], in_=dev[t][:], func=ACT.Sigmoid, bias=minus3[:], scale=slope[:, t : t + 1])

        def move(t):
            nc.vector.scalar_tensor_tensor(out=moved[:, t, :], in0=diff[t][:], scalar=unit_t[:, 2 * t : 2 * t + 1], in1=alp[t][:], op0=ALU.mult, op1=ALU.mult)

        abs_scalar(0)
        subtract(2)
        row_slope(0, 1)
        abs_scalar(1)
        subtract(3)
        row_slope(1, 2)
        gate(0)
        abs_vector(3)
        abs_scalar(2)
        gate(1)
        move(0)
        row_slope(2, 4)
        gate(3)
        gate(2)
        move(1)

        w3_grouped = sb.tile([P, N, PACK], BF16, name="w3_grouped", align_bytes=64)
        nc.scalar.copy(
            out=w3_grouped[:].rearrange("p (c i) t -> p c t i", i=4),
            in_=w3_raw[:].rearrange("p t (c i) -> p c t i", i=4),
        )
        move(3)
        move(2)
        w3_q = quantize(w3_grouped[:].rearrange("p n t -> p (n t)"), N, "w3q")

        hid = []
        for c, (lo, hi) in enumerate(CHUNKS):
            tile = sb.tile([P, hi - lo, PACK], BF16, name="hid%d" % c, align_bytes=64)
            nc.vector.tensor_tensor(
                out=tile[:].rearrange("p (c i) t -> p c t i", i=4),
                in0=moved[:, :, lo:hi].rearrange("p t (c i) -> p c t i", i=4),
                in1=neg_uy[:, :, lo:hi].rearrange("p t (c i) -> p c t i", i=4),
                op=ALU.subtract,
            )
            hid.append(tile)
            if c > 0:
                finish(nc, sb, ps, c - 1, hid, w3_q, quantize, product, out)
        finish(nc, sb, ps, len(CHUNKS) - 1, hid, w3_q, quantize, product, out)


def finish(nc, sb, ps, c, hid, w3_q, quantize, product, out):
    lo, hi = CHUNKS[c]
    codes, plane = quantize(hid[c][:].rearrange("p n t -> p (n t)"), hi - lo, "hidq%d" % c)
    bank = ps.tile([P, S], F32, name="out_bank%d" % c, tag="first%d" % c)
    product(bank[:, 0 : hi - lo], w3_q, codes, plane, True, True)
    result = sb.tile([P, hi - lo], F32, name="result%d" % c)
    nc.scalar.copy(out=result[:], in_=bank[:, 0 : hi - lo])
    nc.sync.dma_start(out=out[:, lo:hi], in_=result[:])
